import numpy as np
import ml_dtypes


def mxq(x, axis, fmt="e4m3"):
    dtype, down = {"e4m3": (ml_dtypes.float8_e4m3fn, 7), "e5m2": (ml_dtypes.float8_e5m2, 14)}[fmt]
    v = np.moveaxis(np.asarray(x, np.float32).astype(ml_dtypes.bfloat16).astype(np.float64), axis, -1)
    blocks = v.reshape(v.shape[:-1] + (-1, 32))
    amax = np.abs(blocks).max(-1, keepdims=True)
    byte = np.maximum(np.where(amax > 0, np.frexp(amax)[1] - 1 + 127, 0) - down, 1)
    scale = np.exp2(byte - 127.0)
    codes = (blocks / scale).astype(np.float32).astype(dtype).astype(np.float64)
    return np.moveaxis((codes * scale).reshape(v.shape), -1, axis)


WIDE = False


def mx_kscale(k):
    if not WIDE:
        return np.ones(k)
    levels = np.array([10, -10, 5, -5, 0])
    if k % 512:
        return np.exp2(np.random.permutation(np.resize(levels, k // 32))).repeat(32)
    a = np.empty((k // 512, 16))
    for p in range(k // 512):
        a[p, :8] = np.random.permutation(np.resize(levels, 8))
        for g in range(8):
            far = levels[np.abs(levels - a[p, g]) >= 10]
            a[p, g + 8] = far[np.random.randint(len(far))]
    return np.exp2(a.ravel()).repeat(32)


def f64(x):
    return np.asarray(x).astype(np.float64)


def striped(idx):
    return np.tile(idx.reshape(-1, 16).T, (8, 1)).astype(np.uint16)


def unstriped(offs):
    return offs[:16].T.reshape(-1).astype(np.int64)


E2M1 = np.array([0.0, 0.5, 1.0, 1.5, 2.0, 3.0, 4.0, 6.0, -0.0, -0.5, -1.0, -1.5, -2.0, -3.0, -4.0, -6.0])


def pack_fp4(w):
    k, n = w.shape
    w = f64(np.asarray(w, np.float32).astype(ml_dtypes.bfloat16)).reshape(k // 32, 32, n)
    amax = np.abs(w).max(1)
    mant, ex = np.frexp(amax / 6.0)
    byte = np.clip(np.where(amax > 0, np.where(mant > 0.5, ex, ex - 1) + 127, 1), 1, 254)
    scaled = (w * np.exp2(127.0 - byte)[:, None, :]).reshape(k, n).astype(np.float32)
    c = np.ascontiguousarray(scaled.reshape(k // 512, 128, 4, n).transpose(0, 1, 3, 2)).astype(ml_dtypes.float4_e2m1fn).view(np.uint8) & 0xF
    words = (c[..., 0::2] | (c[..., 1::2] << 4)).reshape(k // 512, 128, 2 * n)
    return np.ascontiguousarray(words), np.ascontiguousarray(byte.astype(np.uint8).reshape(k // 512, 16, n))


def unpack_fp4(words, scales):
    g, _, n = scales.shape
    words = np.ascontiguousarray(words).reshape(g, 128, n, 2)
    nib = np.empty((g, 128, n, 4), np.uint8)
    nib[..., 0::2] = words & 0xF
    nib[..., 1::2] = words >> 4
    vals = E2M1[nib] * np.repeat(np.exp2(scales.astype(np.float64) - 127.0), 8, axis=1)[..., None]
    return vals.transpose(0, 1, 3, 2).reshape(g * 512, n)


def planes(y):
    n, m = y.shape
    v = y.astype(np.float32).astype(ml_dtypes.bfloat16).astype(np.float64).reshape(n // 32, 32, m)
    top = np.abs(v).max(1)
    byte = np.clip(np.where(top > 0, np.frexp(top)[1] - 1 + 127 - 7, 1), 1, 254)
    codes = (v * np.exp2(127.0 - byte)[:, None, :]).reshape(n, m).astype(np.float32).astype(ml_dtypes.float8_e4m3fn).view(np.uint8)
    words = codes.reshape(n // 512, 128, 4, m).transpose(0, 1, 3, 2)
    return np.ascontiguousarray(words), np.ascontiguousarray(byte.astype(np.uint8).reshape(n // 512, 16, m))


K, T, N = 512, 1024, 512
P = 2 ** 7


def setup_inputs():
    n = np.random.standard_normal
    s = mx_kscale(K)[:, None]
    packed_xT = pack_fp4(n((K, T)) * s)
    return {
        "x_words": packed_xT[0],
        "x_scales": packed_xT[1],
        "w1": (n((K, N)) / np.sqrt(K) / s).astype(np.float32),
        "bound": np.tile(np.random.uniform(0.3, 1.2, T), (P, 1)).astype(np.float32),
        "pos1": striped(np.random.permutation(T)),
        "pos2": striped(np.random.permutation(T)),
        "pos3": striped(np.random.permutation(T)),
        "pos4": striped(np.random.permutation(T)),
    }


def reference(x_words, x_scales, w1, bound, pos1, pos2, pos3, pos4):
    xq = unpack_fp4(x_words, x_scales)
    y = mxq(f64(w1), 0, "e4m3").T @ xq
    low = -1.0 * f64(bound)[:1]
    out_0 = y + (np.maximum(np.minimum(y[:, unstriped(pos1)] - y, f64(bound)[:1]), low) + np.maximum(np.minimum(y[:, unstriped(pos2)] - y, f64(bound)[:1]), low) + np.maximum(np.minimum(y[:, unstriped(pos3)] - y, f64(bound)[:1]), low) + np.maximum(np.minimum(y[:, unstriped(pos4)] - y, f64(bound)[:1]), low)) / 4
    return (out_0,) + planes(out_0)

@@ -1,0 +1,233 @@
+from contextlib import ExitStack
+
+import concourse.mybir as mybir
+from concourse.masks import make_identity
+
+K, T, N = 512, 1024, 512
+FLOPS = 2 * K * T * N
+
+F32 = mybir.dt.float32
+BF16 = mybir.dt.bfloat16
+I32 = mybir.dt.int32
+U32 = mybir.dt.uint32
+U16 = mybir.dt.uint16
+U8 = mybir.dt.uint8
+FP8X4 = mybir.dt.float8_e4m3fn_x4
+FP4X4 = mybir.dt.float4_e2m1fn_x4
+ALU = mybir.AluOpType
+COPY = mybir.ActivationFunctionType.Copy
+
+P = 128
+PACK = 4
+BANK = 512
+LISTS = 4
+
+CHUNKS = [
+    (0, 256, [(0, 1), (2, 3)]),
+    (256, 256, [(0, 1), (2, 3)]),
+    (512, 256, [(0, 1), (2, 3)]),
+    (768, 128, [(0, 1), (2, 3)]),
+    (896, 128, [(0,), (1,), (2,), (3,)]),
+]
+
+
+def tile_picked_whuber_none_lo_kernel(
+    tc, x_words, x_scales, w1, bound, pos1, pos2, pos3, pos4, out_0, out_1, out_2
+):
+    nc = tc.nc
+    with ExitStack() as ctx:
+        keep = ctx.enter_context(tc.tile_pool(name="keep", bufs=1))
+        ring = ctx.enter_context(tc.tile_pool(name="ring", bufs=2))
+        psum = ctx.enter_context(tc.psum_pool(name="psum", bufs=1))
+
+        w_raw = keep.tile([P, PACK, N], F32, name="w_raw")
+        nc.sync.dma_start(out=w_raw[:], in_=w1.rearrange("(p j) c -> p j c", j=PACK))
+
+        x_plane = keep.tile([P, T], U8, name="x_plane", align_bytes=64)
+        nc.vector.memset(x_plane[:].bitcast(I32), 0)
+        for q in range(4):
+            nc.scalar.dma_start(
+                out=x_plane[32 * q : 32 * q + 4, :].bitcast(I32),
+                in_=x_scales[0, 4 * q : 4 * q + 4, :].bitcast(I32),
+            )
+        x_codes = keep.tile([P, 2 * T], U8, name="x_codes", align_bytes=64)
+        nc.sync.dma_start(out=x_codes[:].bitcast(I32), in_=x_words[0].bitcast(I32))
+
+        lists = [keep.tile([P, T // 16], U16, name="list%d" % d) for d in range(LISTS)]
+        nc.sync.dma_start(lists[0][:], pos1)
+
+        bound_rows = keep.tile([P, P], F32, name="bound_rows")
+        nc.vector.memset(bound_rows[:], 0.0)
+        nc.sync.dma_start(
+            out=bound_rows[0 : T // P, :],
+            in_=bound[0:1, :].rearrange("o (c i) -> (o c) i", i=P),
+        )
+        nc.sync.dma_start(lists[1][:], pos2)
+        nc.sync.dma_start(lists[2][:], pos3)
+        nc.sync.dma_start(lists[3][:], pos4)
+
+        ident = keep.tile([P, P], F32, name="ident")
+        make_identity(nc, ident[:])
+
+        def bank():
+            return psum.tile([P, BANK], F32, name="work_bank", tag="work_bank", bufs=5)
+
+        w_bf = [keep.tile([P, P, PACK], BF16, name="w_bf%d" % t, align_bytes=64) for t in range(PACK)]
+        w_codes = [keep.tile([P, P], U32, name="w_codes%d" % t, align_bytes=64) for t in range(PACK)]
+        w_plane = [keep.tile([P, P], U8, name="w_plane%d" % t, align_bytes=64) for t in range(PACK)]
+        dealt = w_raw[:].rearrange("p j (m t) -> p t m j", t=PACK)
+
+        def round_w(t):
+            if t == 1:
+                nc.scalar.copy(out=w_bf[t][:], in_=dealt[:, t, :, :])
+            else:
+                nc.vector.tensor_copy(out=w_bf[t][:], in_=dealt[:, t, :, :])
+
+        def quant_w(t):
+            nc.vector.quantize_mx(
+                out=w_codes[t][:].bitcast(FP8X4),
+                scales=w_plane[t][:],
+                in_=w_bf[t][:].rearrange("p m j -> p (m j)"),
+            )
+
+        y = [keep.tile([P, T], F32, name="y%d" % t) for t in range(PACK)]
+        y_neg = [keep.tile([P, T], F32, name="y_neg%d" % t) for t in range(PACK)]
+
+        def project(t):
+            for h in range(T // BANK):
+                acc = bank()
+                nc.tensor.matmul_mx(
+                    out=acc[:],
+                    lhsT=w_codes[t][:].bitcast(FP8X4),
+                    lhsT_scale=w_plane[t][:],
+                    rhs=x_codes[:, 2 * BANK * h : 2 * BANK * (h + 1)].bitcast(FP4X4),
+                    rhs_scale=x_plane[:, BANK * h : BANK * (h + 1)],
+                    start=True,
+                    stop=True,
+                )
+                cols = slice(BANK * h, BANK * (h + 1))
+                if t == 0 and h == 1:
+                    nc.vector.tensor_copy(out=y[t][:, cols], in_=acc[:])
+                else:
+                    nc.scalar.copy(out=y[t][:, cols], in_=acc[:])
+            nc.gpsimd.tensor_scalar(y_neg[t][:], y[t][:], -1.0, 0.0, ALU.mult, ALU.add)
+
+        bound_t = bank()
+        nc.tensor.transpose(bound_t[:, 0:P], bound_rows[:], ident[:])
+        hi = keep.tile([P, T // P], F32, name="hi")
+        lo = keep.tile([P, T // P], F32, name="lo")
+        nc.scalar.copy(out=hi[:], in_=bound_t[:, 0 : T // P])
+        nc.scalar.activation(out=lo[:], in_=bound_t[:, 0 : T // P], func=COPY, scale=-1.0)
+
+        round_w(0)
+        round_w(1)
+        quant_w(0)
+        project(0)
+        round_w(2)
+        quant_w(1)
+        project(1)
+        round_w(3)
+        quant_w(2)
+        project(2)
+        quant_w(3)
+        project(3)
+
+        out_codes = keep.tile([P, T], U32, name="out_codes", align_bytes=64)
+        out_plane = keep.tile([P, T], U8, name="out_plane", align_bytes=64)
+        out_rows = out_0.rearrange("(p t) v -> p t v", t=PACK)
+        out_words = out_1[0].rearrange("p c r -> p (c r)").bitcast(I32)
+
+        for ci, (v0, n, groups) in enumerate(CHUNKS):
+            blocks = n // P
+            last_chunk = ci == len(CHUNKS) - 1
+            res = keep.tile([P, PACK, n], F32, name="res%d" % ci)
+            for group in groups:
+                on_vector = last_chunk and group[0] >= 2
+                picked = {}
+                for t in group:
+                    for d in range(LISTS):
+                        g = keep.tile([P, n], F32, name="picked%d_%d_%d" % (ci, t, d))
+                        nc.vector.tensor_copy(
+                            g[:], y[t][:].indirect(lists[d][:, v0 // 16 : (v0 + n) // 16])
+                        )
+                        picked[t, d] = g
+                clipped = [
+                    ring.tile([P, len(group), BANK], F32, name="clipped", tag="clipped", bufs=5)
+                    for b in range(blocks)
+                ]
+                if not on_vector:
+                    pulls = [
+                        ring.tile([P, len(group), BANK], F32, name="pulls", tag="pulls", bufs=4)
+                        for b in range(blocks)
+                    ]
+                for i, t in enumerate(group):
+                    for b in range(blocks):
+                        vb = v0 // P + b
+                        u = bank()
+                        for d in range(LISTS):
+                            nc.tensor.matmul(
+                                u[:, P * d : P * (d + 1)], y_neg[t][:, P * vb : P * (vb + 1)], ident[:],
+                                start=(d == 0), stop=False, is_transpose=True,
+                            )
+                        for d in range(LISTS):
+                            nc.tensor.matmul(
+                                u[:, P * d : P * (d + 1)], picked[t, d][:, P * b : P * (b + 1)], ident[:],
+                                start=False, stop=(d == LISTS - 1), is_transpose=True,
+                            )
+                        if on_vector:
+                            nc.vector.tensor_scalar(
+                                clipped[b][:, i, :], u[:], hi[:, vb : vb + 1], lo[:, vb : vb + 1], ALU.min, ALU.max
+                            )
+                        else:
+                            nc.scalar.copy(out=pulls[b][:, i, :], in_=u[:])
+                if not on_vector:
+                    for b in range(blocks):
+                        vb = v0 // P + b
+                        nc.gpsimd.tensor_scalar(
+                            clipped[b][:].rearrange("p i c -> p (i c)"),
+                            pulls[b][:].rearrange("p i c -> p (i c)"),
+                            hi[:, vb : vb + 1], lo[:, vb : vb + 1], ALU.min, ALU.max,
+                        )
+                for i, t in enumerate(group):
+                    total = psum.tile([P, n], F32, name="sum_bank", tag="sum_bank", bufs=3)
+                    for b in range(blocks):
+                        for d in range(LISTS):
+                            nc.tensor.matmul(
+                                total[:, P * b : P * (b + 1)],
+                                clipped[b][:, i, P * d : P * (d + 1)], ident[:],
+                                start=(d == 0), stop=(d == LISTS - 1), is_transpose=True,
+                            )
+                    if last_chunk:
+                        nc.vector.scalar_tensor_tensor(
+                            res[:, t, :], total[:], 1.0 / LISTS, y[t][:, v0 : v0 + n], ALU.mult, ALU.add
+                        )
+                    else:
+                        mean = ring.tile([P, n], F32, name="mean", tag="mean", bufs=3)
+                        nc.scalar.activation(out=mean[:], in_=total[:], func=COPY, scale=1.0 / LISTS)
+                        nc.gpsimd.tensor_tensor(res[:, t, :], mean[:], y[t][:, v0 : v0 + n], ALU.add)
+                if not last_chunk:
+                    ts = slice(group[0], group[-1] + 1)
+                    nc.sync.dma_start(out=out_rows[:, ts, v0 : v0 + n], in_=res[:, ts, :])
+            if last_chunk:
+                nc.sync.dma_start(out=out_rows[:, :, v0 : v0 + n], in_=res[:])
+
+            woven = keep.tile([P, n, PACK], BF16, name="woven%d" % ci, align_bytes=64)
+            dst = woven[:].rearrange("p (c i) t -> p c t i", i=4)
+            src = res[:].rearrange("p t (c i) -> p c t i", i=4)
+            if last_chunk:
+                nc.vector.tensor_copy(out=dst, in_=src)
+            else:
+                nc.scalar.copy(out=dst, in_=src)
+            nc.vector.quantize_mx(
+                out=out_codes[:, v0 : v0 + n].bitcast(FP8X4),
+                scales=out_plane[:, v0 : v0 + n],
+                in_=woven[:].rearrange("p c t -> p (c t)"),
+            )
+            nc.sync.dma_start(out=out_words[:, v0 : v0 + n], in_=out_codes[:, v0 : v0 + n].bitcast(I32))
+
+        for q in range(4):
+            queue = nc.scalar if q % 2 == 0 else nc.sync
+            queue.dma_start(
+                out=out_2[0, 4 * q : 4 * q + 4, :].bitcast(I32),
+                in_=out_plane[32 * q : 32 * q + 4, :].bitcast(I32),
+            )

@@ -91,7 +91,7 @@ def tile_picked_whuber_none_lo_kernel(
             )
 
         y = [keep.tile([P, T], F32, name="y%d" % t) for t in range(PACK)]
-        y_neg = [keep.tile([P, T], F32, name="y_neg%d" % t) for t in range(PACK)]
+        y_neg = keep.tile([P, PACK, T], F32, name="y_neg")
 
         def project(t):
             for h in range(T // BANK):
@@ -110,7 +110,7 @@ def tile_picked_whuber_none_lo_kernel(
                     nc.vector.tensor_copy(out=y[t][:, cols], in_=acc[:])
                 else:
                     nc.scalar.copy(out=y[t][:, cols], in_=acc[:])
-            nc.gpsimd.tensor_scalar(y_neg[t][:], y[t][:], -1.0, 0.0, ALU.mult, ALU.add)
+            nc.gpsimd.tensor_scalar(y_neg[:, t, :], y[t][:], -1.0, 0.0, ALU.mult, ALU.add)
 
         bound_t = bank()
         nc.tensor.transpose(bound_t[:, 0:P], bound_rows[:], ident[:])
@@ -137,93 +137,122 @@ def tile_picked_whuber_none_lo_kernel(
         out_rows = out_0.rearrange("(p t) v -> p t v", t=PACK)
         out_words = out_1[0].rearrange("p c r -> p (c r)").bitcast(I32)
 
-        for ci, (v0, n, groups) in enumerate(CHUNKS):
+        last = len(CHUNKS) - 1
+        res = [keep.tile([P, PACK, n], F32, name="res%d" % ci) for ci, (v0, n, groups) in enumerate(CHUNKS)]
+
+        y_turned = [keep.tile([P, T], F32, name="y_turned%d" % t) for t in range(PACK)]
+
+        def turn_y(t):
+            for h in range(T // BANK):
+                turned = bank()
+                for b in range(BANK // P):
+                    vb = h * (BANK // P) + b
+                    nc.tensor.transpose(turned[:, P * b : P * (b + 1)], y[t][:, P * vb : P * (vb + 1)], ident[:])
+                nc.scalar.activation(
+                    out=y_turned[t][:, BANK * h : BANK * (h + 1)], in_=turned[:], func=COPY, scale=float(LISTS)
+                )
+
+        def forward(ci, group):
+            v0, n, groups = CHUNKS[ci]
             blocks = n // P
-            last_chunk = ci == len(CHUNKS) - 1
-            res = keep.tile([P, PACK, n], F32, name="res%d" % ci)
-            for group in groups:
-                on_vector = last_chunk and group[0] >= 2
-                picked = {}
-                for t in group:
-                    for d in range(LISTS):
-                        g = keep.tile([P, n], F32, name="picked%d_%d_%d" % (ci, t, d))
-                        nc.vector.tensor_copy(
-                            g[:], y[t][:].indirect(lists[d][:, v0 // 16 : (v0 + n) // 16])
-                        )
-                        picked[t, d] = g
-                clipped = [
-                    ring.tile([P, len(group), BANK], F32, name="clipped", tag="clipped", bufs=5)
+            on_vector = ci == last and group[0] >= 2
+            picked = {}
+            for t in group:
+                for d in range(LISTS):
+                    g = keep.tile([P, n], F32, name="picked%d_%d_%d" % (ci, t, d))
+                    nc.vector.tensor_copy(g[:], y[t][:].indirect(lists[d][:, v0 // 16 : (v0 + n) // 16]))
+                    picked[t, d] = g
+            clipped = [
+                ring.tile([P, len(group), BANK], F32, name="clipped", tag="clipped", bufs=6)
+                for b in range(blocks)
+            ]
+            if not on_vector:
+                pulls = [
+                    ring.tile([P, len(group), BANK], F32, name="pulls", tag="pulls", bufs=4)
                     for b in range(blocks)
                 ]
-                if not on_vector:
-                    pulls = [
-                        ring.tile([P, len(group), BANK], F32, name="pulls", tag="pulls", bufs=4)
-                        for b in range(blocks)
-                    ]
-                for i, t in enumerate(group):
-                    for b in range(blocks):
-                        vb = v0 // P + b
-                        u = bank()
-                        for d in range(LISTS):
-                            nc.tensor.matmul(
-                                u[:, P * d : P * (d + 1)], y_neg[t][:, P * vb : P * (vb + 1)], ident[:],
-                                start=(d == 0), stop=False, is_transpose=True,
-                            )
-                        for d in range(LISTS):
-                            nc.tensor.matmul(
-                                u[:, P * d : P * (d + 1)], picked[t, d][:, P * b : P * (b + 1)], ident[:],
-                                start=False, stop=(d == LISTS - 1), is_transpose=True,
-                            )
-                        if on_vector:
-                            nc.vector.tensor_scalar(
-                                clipped[b][:, i, :], u[:], hi[:, vb : vb + 1], lo[:, vb : vb + 1], ALU.min, ALU.max
-                            )
-                        else:
-                            nc.scalar.copy(out=pulls[b][:, i, :], in_=u[:])
-                if not on_vector:
-                    for b in range(blocks):
-                        vb = v0 // P + b
-                        nc.gpsimd.tensor_scalar(
-                            clipped[b][:].rearrange("p i c -> p (i c)"),
-                            pulls[b][:].rearrange("p i c -> p (i c)"),
-                            hi[:, vb : vb + 1], lo[:, vb : vb + 1], ALU.min, ALU.max,
+            for i, t in enumerate(group):
+                for b in range(blocks):
+                    vb = v0 // P + b
+                    u = bank()
+                    for d in range(LISTS):
+                        nc.tensor.matmul(
+                            u[:, P * d : P * (d + 1)], y_neg[:, t, P * vb : P * (vb + 1)], ident[:],
+                            start=(d == 0), stop=False, is_transpose=True,
                         )
-                for i, t in enumerate(group):
-                    total = psum.tile([P, n], F32, name="sum_bank", tag="sum_bank", bufs=3)
-                    for b in range(blocks):
-                        for d in range(LISTS):
-                            nc.tensor.matmul(
-                                total[:, P * b : P * (b + 1)],
-                                clipped[b][:, i, P * d : P * (d + 1)], ident[:],
-                                start=(d == 0), stop=(d == LISTS - 1), is_transpose=True,
-                            )
-                    if last_chunk:
-                        nc.vector.scalar_tensor_tensor(
-                            res[:, t, :], total[:], 1.0 / LISTS, y[t][:, v0 : v0 + n], ALU.mult, ALU.add
+                    for d in range(LISTS):
+                        nc.tensor.matmul(
+                            u[:, P * d : P * (d + 1)], picked[t, d][:, P * b : P * (b + 1)], ident[:],
+                            start=False, stop=(d == LISTS - 1), is_transpose=True,
+                        )
+                    if on_vector:
+                        nc.vector.tensor_scalar(
+                            clipped[b][:, i, :], u[:], hi[:, vb : vb + 1], lo[:, vb : vb + 1], ALU.min, ALU.max
                         )
                     else:
-                        mean = ring.tile([P, n], F32, name="mean", tag="mean", bufs=3)
-                        nc.scalar.activation(out=mean[:], in_=total[:], func=COPY, scale=1.0 / LISTS)
-                        nc.gpsimd.tensor_tensor(res[:, t, :], mean[:], y[t][:, v0 : v0 + n], ALU.add)
-                if not last_chunk:
-                    ts = slice(group[0], group[-1] + 1)
-                    nc.sync.dma_start(out=out_rows[:, ts, v0 : v0 + n], in_=res[:, ts, :])
-            if last_chunk:
-                nc.sync.dma_start(out=out_rows[:, :, v0 : v0 + n], in_=res[:])
+                        nc.scalar.copy(out=pulls[b][:, i, :], in_=u[:])
+                if ci == 0:
+                    turn_y(t)
+            if not on_vector:
+                for b in range(blocks):
+                    vb = v0 // P + b
+                    nc.gpsimd.tensor_scalar(
+                        clipped[b][:].rearrange("p i c -> p (i c)"),
+                        pulls[b][:].rearrange("p i c -> p (i c)"),
+                        hi[:, vb : vb + 1], lo[:, vb : vb + 1], ALU.min, ALU.max,
+                    )
+            return clipped
 
-            woven = keep.tile([P, n, PACK], BF16, name="woven%d" % ci, align_bytes=64)
-            dst = woven[:].rearrange("p (c i) t -> p c t i", i=4)
-            src = res[:].rearrange("p t (c i) -> p c t i", i=4)
-            if last_chunk:
-                nc.vector.tensor_copy(out=dst, in_=src)
-            else:
-                nc.scalar.copy(out=dst, in_=src)
-            nc.vector.quantize_mx(
-                out=out_codes[:, v0 : v0 + n].bitcast(FP8X4),
-                scales=out_plane[:, v0 : v0 + n],
-                in_=woven[:].rearrange("p c t -> p (c t)"),
-            )
-            nc.sync.dma_start(out=out_words[:, v0 : v0 + n], in_=out_codes[:, v0 : v0 + n].bitcast(I32))
+        def backward(ci, group, clipped):
+            v0, n, groups = CHUNKS[ci]
+            blocks = n // P
+            ts = slice(group[0], group[-1] + 1)
+            total = psum.tile([P, len(group), n], F32, name="sum_bank", tag="sum_bank", bufs=3)
+            for i, t in enumerate(group):
+                for b in range(blocks):
+                    vb = v0 // P + b
+                    nc.tensor.matmul(
+                        total[:, i, P * b : P * (b + 1)], y_turned[t][:, P * vb : P * (vb + 1)], ident[:],
+                        start=True, stop=False, is_transpose=True,
+                    )
+                    for d in range(LISTS):
+                        nc.tensor.matmul(
+                            total[:, i, P * b : P * (b + 1)],
+                            clipped[b][:, i, P * d : P * (d + 1)], ident[:],
+                            start=False, stop=(d == LISTS - 1), is_transpose=True,
+                        )
+            nc.scalar.activation(out=res[ci][:, ts, :], in_=total[:], func=COPY, scale=1.0 / LISTS)
+            if ci != last:
+                nc.sync.dma_start(out=out_rows[:, ts, v0 : v0 + n], in_=res[ci][:, ts, :])
+            if group == groups[-1]:
+                if ci == last:
+                    nc.sync.dma_start(out=out_rows[:, :, v0 : v0 + n], in_=res[ci][:])
+                woven = keep.tile([P, n, PACK], BF16, name="woven%d" % ci, align_bytes=64)
+                dst = woven[:].rearrange("p (c i) t -> p c t i", i=4)
+                src = res[ci][:].rearrange("p t (c i) -> p c t i", i=4)
+                if ci == last:
+                    nc.vector.tensor_copy(out=dst, in_=src)
+                else:
+                    nc.scalar.copy(out=dst, in_=src)
+                nc.vector.quantize_mx(
+                    out=out_codes[:, v0 : v0 + n].bitcast(FP8X4),
+                    scales=out_plane[:, v0 : v0 + n],
+                    in_=woven[:].rearrange("p c t -> p (c t)"),
+                )
+                if ci >= last - 1:
+                    first = 0 if ci < last else v0
+                    nc.sync.dma_start(
+                        out=out_words[:, first : v0 + n], in_=out_codes[:, first : v0 + n].bitcast(I32)
+                    )
+
+        steps = [(ci, group) for ci, (v0, n, groups) in enumerate(CHUNKS) for group in groups]
+        waiting = None
+        for ci, group in steps:
+            clipped = forward(ci, group)
+            if waiting is not None:
+                backward(*waiting)
+            waiting = (ci, group, clipped)
+        backward(*waiting)
 
         for q in range(4):
             queue = nc.scalar if q % 2 == 0 else nc.sync

@@ -23,8 +23,7 @@ BANK = 512
 LISTS = 4
 
 CHUNKS = [
-    (0, 256, [(0, 1), (2, 3)]),
-    (256, 256, [(0, 1), (2, 3)]),
+    (0, 512, [(0,), (1,), (2,), (3,)]),
     (512, 256, [(0, 1), (2, 3)]),
     (768, 128, [(0, 1), (2, 3)]),
     (896, 128, [(0,), (1,), (2,), (3,)]),
@@ -40,13 +39,15 @@ def tile_picked_whuber_none_lo_kernel(
         ring = ctx.enter_context(tc.tile_pool(name="ring", bufs=2))
         psum = ctx.enter_context(tc.psum_pool(name="psum", bufs=1))
 
-        w_raw = keep.tile([P, PACK, N], F32, name="w_raw")
-        nc.sync.dma_start(out=w_raw[:], in_=w1.rearrange("(p j) c -> p j c", j=PACK))
+        w_rows = w1.rearrange("(p j) c -> p j c", j=PACK)
+        w_raw = [keep.tile([P, PACK, N // 2], F32, name="w_raw%d" % h) for h in range(2)]
+        for h in range(2):
+            nc.sync.dma_start(out=w_raw[h][:], in_=w_rows[:, :, h * (N // 2) : (h + 1) * (N // 2)])
 
         x_plane = keep.tile([P, T], U8, name="x_plane", align_bytes=64)
-        nc.vector.memset(x_plane[:].bitcast(I32), 0)
+        nc.gpsimd.memset(x_plane[:].bitcast(I32), 0)
         for q in range(4):
-            nc.scalar.dma_start(
+            nc.sync.dma_start(
                 out=x_plane[32 * q : 32 * q + 4, :].bitcast(I32),
                 in_=x_scales[0, 4 * q : 4 * q + 4, :].bitcast(I32),
             )
@@ -58,13 +59,13 @@ def tile_picked_whuber_none_lo_kernel(
 
         bound_rows = keep.tile([P, P], F32, name="bound_rows")
         nc.vector.memset(bound_rows[:], 0.0)
+        nc.sync.dma_start(lists[1][:], pos2)
+        nc.sync.dma_start(lists[2][:], pos3)
+        nc.sync.dma_start(lists[3][:], pos4)
         nc.sync.dma_start(
             out=bound_rows[0 : T // P, :],
             in_=bound[0:1, :].rearrange("o (c i) -> (o c) i", i=P),
         )
-        nc.sync.dma_start(lists[1][:], pos2)
-        nc.sync.dma_start(lists[2][:], pos3)
-        nc.sync.dma_start(lists[3][:], pos4)
 
         ident = keep.tile([P, P], F32, name="ident")
         make_identity(nc, ident[:])
@@ -72,45 +73,61 @@ def tile_picked_whuber_none_lo_kernel(
         def bank():
             return psum.tile([P, BANK], F32, name="work_bank", tag="work_bank", bufs=5)
 
-        w_bf = [keep.tile([P, P, PACK], BF16, name="w_bf%d" % t, align_bytes=64) for t in range(PACK)]
+        w_bf = [keep.tile([P, P, PACK], BF16, name="w_bf%d" % t, align_bytes=64)[:] for t in range(2)]
+        w_bf_pair = keep.tile([P, 2, P, PACK], BF16, name="w_bf_pair", align_bytes=64)
+        w_bf = w_bf + [w_bf_pair[:, 0, :, :], w_bf_pair[:, 1, :, :]]
         w_codes = [keep.tile([P, P], U32, name="w_codes%d" % t, align_bytes=64) for t in range(PACK)]
         w_plane = [keep.tile([P, P], U8, name="w_plane%d" % t, align_bytes=64) for t in range(PACK)]
-        dealt = w_raw[:].rearrange("p j (m t) -> p t m j", t=PACK)
+        dealt = [w_raw[h][:].rearrange("p j (m t) -> p t m j", t=PACK) for h in range(2)]
+        halves = [slice(0, P // 2), slice(P // 2, P)]
 
-        def round_w(t):
-            if t == 1:
-                nc.scalar.copy(out=w_bf[t][:], in_=dealt[:, t, :, :])
-            else:
-                nc.vector.tensor_copy(out=w_bf[t][:], in_=dealt[:, t, :, :])
 
         def quant_w(t):
             nc.vector.quantize_mx(
                 out=w_codes[t][:].bitcast(FP8X4),
                 scales=w_plane[t][:],
-                in_=w_bf[t][:].rearrange("p m j -> p (m j)"),
+                in_=w_bf[t].rearrange("p m j -> p (m j)"),
             )
 
         y = [keep.tile([P, T], F32, name="y%d" % t) for t in range(PACK)]
-        y_neg = keep.tile([P, PACK, T], F32, name="y_neg")
+        first = CHUNKS[0][1]
+        own_first = [keep.tile([P, first], F32, name="own_first%d" % t) for t in range(PACK)]
+        own_rest = [keep.tile([P, T - first], F32, name="own_rest%d" % t) for t in range(PACK)]
 
         def project(t):
-            for h in range(T // BANK):
+            width = BANK // 2 if t == 0 else BANK
+            for c0 in range(0, T, width):
+                cols = slice(c0, c0 + width)
                 acc = bank()
                 nc.tensor.matmul_mx(
-                    out=acc[:],
+                    out=acc[:, 0:width],
                     lhsT=w_codes[t][:].bitcast(FP8X4),
                     lhsT_scale=w_plane[t][:],
-                    rhs=x_codes[:, 2 * BANK * h : 2 * BANK * (h + 1)].bitcast(FP4X4),
-                    rhs_scale=x_plane[:, BANK * h : BANK * (h + 1)],
+                    rhs=x_codes[:, 2 * c0 : 2 * (c0 + width)].bitcast(FP4X4),
+                    rhs_scale=x_plane[:, cols],
                     start=True,
                     stop=True,
                 )
-                cols = slice(BANK * h, BANK * (h + 1))
-                if t == 0 and h == 1:
-                    nc.vector.tensor_copy(out=y[t][:, cols], in_=acc[:])
+                if t == 0 and c0 >= first:
+                    nc.vector.tensor_copy(out=y[t][:, cols], in_=acc[:, 0:width])
                 else:
-                    nc.scalar.copy(out=y[t][:, cols], in_=acc[:])
-            nc.gpsimd.tensor_scalar(y_neg[:, t, :], y[t][:], -1.0, 0.0, ALU.mult, ALU.add)
+                    nc.scalar.copy(out=y[t][:, cols], in_=acc[:, 0:width])
+                if c0 < first:
+                    nc.scalar.copy(out=own_first[t][:, cols], in_=acc[:, 0:width])
+            nc.sync.dma_start(out=own_rest[t][:], in_=y[t][:, first:T])
+
+        for h in range(2):
+            nc.vector.tensor_copy(out=w_bf[0][:, halves[h], :], in_=dealt[h][:, 0, :, :])
+            nc.scalar.copy(out=w_bf[1][:, halves[h], :], in_=dealt[h][:, 1, :, :])
+        quant_w(0)
+        for h in range(2):
+            nc.vector.tensor_copy(
+                out=w_bf_pair[:, :, halves[h], :].rearrange("p t m j -> p m t j"),
+                in_=dealt[h][:, 2:4, :, :].rearrange("p t m j -> p m t j"),
+            )
+        project(0)
+        quant_w(1)
+        project(1)
 
         bound_t = bank()
         nc.tensor.transpose(bound_t[:, 0:P], bound_rows[:], ident[:])
@@ -119,18 +136,6 @@ def tile_picked_whuber_none_lo_kernel(
         nc.scalar.copy(out=hi[:], in_=bound_t[:, 0 : T // P])
         nc.scalar.activation(out=lo[:], in_=bound_t[:, 0 : T // P], func=COPY, scale=-1.0)
 
-        round_w(0)
-        round_w(1)
-        quant_w(0)
-        project(0)
-        round_w(2)
-        quant_w(1)
-        project(1)
-        round_w(3)
-        quant_w(2)
-        project(2)
-        quant_w(3)
-        project(3)
 
         out_codes = keep.tile([P, T], U32, name="out_codes", align_bytes=64)
         out_plane = keep.tile([P, T], U8, name="out_plane", align_bytes=64)
@@ -155,52 +160,47 @@ def tile_picked_whuber_none_lo_kernel(
         def forward(ci, group):
             v0, n, groups = CHUNKS[ci]
             blocks = n // P
-            on_vector = ci == last and group[0] >= 2
+            on_vector = ci == last and group[0] == 3
             picked = {}
             for t in group:
                 for d in range(LISTS):
-                    g = keep.tile([P, n], F32, name="picked%d_%d_%d" % (ci, t, d))
-                    nc.vector.tensor_copy(g[:], y[t][:].indirect(lists[d][:, v0 // 16 : (v0 + n) // 16]))
+                    g = ring.tile([P, n], F32, name="picked", tag="picked", bufs=8)
+                    own = own_first[t][:] if ci == 0 else own_rest[t][:, v0 - first : v0 - first + n]
+                    nc.vector.tensor_tensor(
+                        g[:], y[t][:].indirect(lists[d][:, v0 // 16 : (v0 + n) // 16]), own, ALU.subtract
+                    )
                     picked[t, d] = g
             clipped = [
-                ring.tile([P, len(group), BANK], F32, name="clipped", tag="clipped", bufs=6)
+                ring.tile([P, len(group), BANK], F32, name="clipped", tag="clipped", bufs=10)
                 for b in range(blocks)
             ]
-            if not on_vector:
-                pulls = [
-                    ring.tile([P, len(group), BANK], F32, name="pulls", tag="pulls", bufs=4)
-                    for b in range(blocks)
-                ]
+            pulls = [
+                ring.tile([P, len(group), BANK], F32, name="pulls", tag="pulls", bufs=6)
+                for b in range(blocks)
+            ]
+            staged = LISTS - 1 if on_vector else LISTS
             for i, t in enumerate(group):
                 for b in range(blocks):
-                    vb = v0 // P + b
                     u = bank()
-                    for d in range(LISTS):
-                        nc.tensor.matmul(
-                            u[:, P * d : P * (d + 1)], y_neg[:, t, P * vb : P * (vb + 1)], ident[:],
-                            start=(d == 0), stop=False, is_transpose=True,
-                        )
-                    for d in range(LISTS):
-                        nc.tensor.matmul(
-                            u[:, P * d : P * (d + 1)], picked[t, d][:, P * b : P * (b + 1)], ident[:],
-                            start=False, stop=(d == LISTS - 1), is_transpose=True,
-                        )
-                    if on_vector:
-                        nc.vector.tensor_scalar(
-                            clipped[b][:, i, :], u[:], hi[:, vb : vb + 1], lo[:, vb : vb + 1], ALU.min, ALU.max
-                        )
-                    else:
-                        nc.scalar.copy(out=pulls[b][:, i, :], in_=u[:])
+                    for d in range(staged):
+                        nc.tensor.transpose(u[:, P * d : P * (d + 1)], picked[t, d][:, P * b : P * (b + 1)], ident[:])
+                    nc.scalar.copy(out=pulls[b][:, i, 0 : P * staged], in_=u[:, 0 : P * staged])
                 if ci == 0:
                     turn_y(t)
-            if not on_vector:
-                for b in range(blocks):
-                    vb = v0 // P + b
-                    nc.gpsimd.tensor_scalar(
-                        clipped[b][:].rearrange("p i c -> p (i c)"),
-                        pulls[b][:].rearrange("p i c -> p (i c)"),
-                        hi[:, vb : vb + 1], lo[:, vb : vb + 1], ALU.min, ALU.max,
-                    )
+            for b in range(blocks):
+                vb = v0 // P + b
+                nc.vector.tensor_scalar(
+                    clipped[b][:].rearrange("p i c -> p (i c)")[:, 0 : len(group) * P * staged],
+                    pulls[b][:].rearrange("p i c -> p (i c)")[:, 0 : len(group) * P * staged],
+                    hi[:, vb : vb + 1], lo[:, vb : vb + 1], ALU.min, ALU.max,
+                )
+            if on_vector:
+                u = bank()
+                nc.tensor.transpose(u[:, 0:P], picked[group[0], staged][:], ident[:])
+                nc.vector.tensor_scalar(
+                    clipped[0][:, 0, P * staged : BANK], u[:, 0:P],
+                    hi[:, vb : vb + 1], lo[:, vb : vb + 1], ALU.min, ALU.max,
+                )
             return clipped
 
         def backward(ci, group, clipped):
@@ -222,11 +222,8 @@ def tile_picked_whuber_none_lo_kernel(
                             start=False, stop=(d == LISTS - 1), is_transpose=True,
                         )
             nc.scalar.activation(out=res[ci][:, ts, :], in_=total[:], func=COPY, scale=1.0 / LISTS)
-            if ci != last:
-                nc.sync.dma_start(out=out_rows[:, ts, v0 : v0 + n], in_=res[ci][:, ts, :])
+            nc.sync.dma_start(out=out_rows[:, ts, v0 : v0 + n], in_=res[ci][:, ts, :])
             if group == groups[-1]:
-                if ci == last:
-                    nc.sync.dma_start(out=out_rows[:, :, v0 : v0 + n], in_=res[ci][:])
                 woven = keep.tile([P, n, PACK], BF16, name="woven%d" % ci, align_bytes=64)
                 dst = woven[:].rearrange("p (c i) t -> p c t i", i=4)
                 src = res[ci][:].rearrange("p t (c i) -> p c t i", i=4)
@@ -234,25 +231,31 @@ def tile_picked_whuber_none_lo_kernel(
                     nc.vector.tensor_copy(out=dst, in_=src)
                 else:
                     nc.scalar.copy(out=dst, in_=src)
-                nc.vector.quantize_mx(
-                    out=out_codes[:, v0 : v0 + n].bitcast(FP8X4),
-                    scales=out_plane[:, v0 : v0 + n],
-                    in_=woven[:].rearrange("p c t -> p (c t)"),
-                )
+                for c0, c1 in ((0, 256), (256, 384)) if n == 384 else ((0, n),):
+                    nc.vector.quantize_mx(
+                        out=out_codes[:, v0 + c0 : v0 + c1].bitcast(FP8X4),
+                        scales=out_plane[:, v0 + c0 : v0 + c1],
+                        in_=woven[:, c0:c1, :].rearrange("p c t -> p (c t)"),
+                    )
                 if ci >= last - 1:
-                    first = 0 if ci < last else v0
+                    c0 = 0 if ci < last else v0
                     nc.sync.dma_start(
-                        out=out_words[:, first : v0 + n], in_=out_codes[:, first : v0 + n].bitcast(I32)
+                        out=out_words[:, c0 : v0 + n], in_=out_codes[:, c0 : v0 + n].bitcast(I32)
                     )
 
         steps = [(ci, group) for ci, (v0, n, groups) in enumerate(CHUNKS) for group in groups]
-        waiting = None
+        begun = []
+        finished = 0
         for ci, group in steps:
-            clipped = forward(ci, group)
-            if waiting is not None:
-                backward(*waiting)
-            waiting = (ci, group, clipped)
-        backward(*waiting)
+            begun.append((ci, group, forward(ci, group)))
+            if ci == 0 and group[0] < 2:
+                quant_w(group[0] + 2)
+                project(group[0] + 2)
+            if len(begun) - finished > (2 if ci == last else 1):
+                backward(*begun[finished])
+                finished = finished + 1
+        for item in begun[finished:]:
+            backward(*item)
 
         for q in range(4):
             queue = nc.scalar if q % 2 == 0 else nc.sync

@@ -21,13 +21,33 @@ P = 128
 PACK = 4
 BANK = 512
 LISTS = 4
+QUADRANTS = 4
 
 CHUNKS = [
-    (0, 512, [(0,), (1,), (2,), (3,)]),
-    (512, 256, [(0, 1), (2, 3)]),
-    (768, 128, [(0, 1), (2, 3)]),
+    (0, 512, [(0, 1), (2,), (3,)]),
+    (512, 384, [(0, 1), (2,), (3,)]),
     (896, 128, [(0,), (1,), (2,), (3,)]),
 ]
+LAST = len(CHUNKS) - 1
+FIRST_WIDTH = CHUNKS[0][1]
+
+PULL_BUFS = 2 * LISTS
+TURNED_BUFS = 2 * (FIRST_WIDTH // P)
+CLIPPED_BUFS = TURNED_BUFS + 2
+WORK_BANKS = 5
+SUM_BANKS = 3
+
+
+def power_of_two_runs(n):
+    runs = []
+    start = 0
+    while start < n:
+        width = 1
+        while 2 * width <= n - start:
+            width = 2 * width
+        runs.append((start, start + width))
+        start = start + width
+    return runs
 
 
 def tile_picked_whuber_none_lo_kernel(
@@ -46,7 +66,7 @@ def tile_picked_whuber_none_lo_kernel(
 
         x_plane = keep.tile([P, T], U8, name="x_plane", align_bytes=64)
         nc.gpsimd.memset(x_plane[:].bitcast(I32), 0)
-        for q in range(4):
+        for q in range(QUADRANTS):
             nc.sync.dma_start(
                 out=x_plane[32 * q : 32 * q + 4, :].bitcast(I32),
                 in_=x_scales[0, 4 * q : 4 * q + 4, :].bitcast(I32),
@@ -70,35 +90,33 @@ def tile_picked_whuber_none_lo_kernel(
         ident = keep.tile([P, P], F32, name="ident")
         make_identity(nc, ident[:])
 
-        def bank():
-            return psum.tile([P, BANK], F32, name="work_bank", tag="work_bank", bufs=5)
+        def work_bank():
+            return psum.tile([P, BANK], F32, name="work_bank", tag="work_bank", bufs=WORK_BANKS)
 
         w_bf = [keep.tile([P, P, PACK], BF16, name="w_bf%d" % t, align_bytes=64)[:] for t in range(2)]
         w_bf_pair = keep.tile([P, 2, P, PACK], BF16, name="w_bf_pair", align_bytes=64)
         w_bf = w_bf + [w_bf_pair[:, 0, :, :], w_bf_pair[:, 1, :, :]]
         w_codes = [keep.tile([P, P], U32, name="w_codes%d" % t, align_bytes=64) for t in range(PACK)]
         w_plane = [keep.tile([P, P], U8, name="w_plane%d" % t, align_bytes=64) for t in range(PACK)]
-        dealt = [w_raw[h][:].rearrange("p j (m t) -> p t m j", t=PACK) for h in range(2)]
+        dealt = [w_raw[h][:].rearrange("p j (i t) -> p t i j", t=PACK) for h in range(2)]
         halves = [slice(0, P // 2), slice(P // 2, P)]
 
-
-        def quant_w(t):
+        def quantise_w(t):
             nc.vector.quantize_mx(
                 out=w_codes[t][:].bitcast(FP8X4),
                 scales=w_plane[t][:],
-                in_=w_bf[t].rearrange("p m j -> p (m j)"),
+                in_=w_bf[t].rearrange("p i j -> p (i j)"),
             )
 
         y = [keep.tile([P, T], F32, name="y%d" % t) for t in range(PACK)]
-        first = CHUNKS[0][1]
-        own_first = [keep.tile([P, first], F32, name="own_first%d" % t) for t in range(PACK)]
-        own_rest = [keep.tile([P, T - first], F32, name="own_rest%d" % t) for t in range(PACK)]
+        own_first = [keep.tile([P, FIRST_WIDTH], F32, name="own_first%d" % t) for t in range(PACK)]
+        own_rest = [keep.tile([P, T - FIRST_WIDTH], F32, name="own_rest%d" % t) for t in range(PACK)]
 
         def project(t):
             width = BANK // 2 if t == 0 else BANK
             for c0 in range(0, T, width):
                 cols = slice(c0, c0 + width)
-                acc = bank()
+                acc = work_bank()
                 nc.tensor.matmul_mx(
                     out=acc[:, 0:width],
                     lhsT=w_codes[t][:].bitcast(FP8X4),
@@ -108,156 +126,152 @@ def tile_picked_whuber_none_lo_kernel(
                     start=True,
                     stop=True,
                 )
-                if t == 0 and c0 >= first:
+                if t == 0 and c0 >= FIRST_WIDTH:
                     nc.vector.tensor_copy(out=y[t][:, cols], in_=acc[:, 0:width])
                 else:
                     nc.scalar.copy(out=y[t][:, cols], in_=acc[:, 0:width])
-                if c0 < first:
+                if c0 < FIRST_WIDTH:
                     nc.scalar.copy(out=own_first[t][:, cols], in_=acc[:, 0:width])
-            nc.sync.dma_start(out=own_rest[t][:], in_=y[t][:, first:T])
+            nc.sync.dma_start(out=own_rest[t][:], in_=y[t][:, FIRST_WIDTH:T])
 
         for h in range(2):
             nc.vector.tensor_copy(out=w_bf[0][:, halves[h], :], in_=dealt[h][:, 0, :, :])
             nc.scalar.copy(out=w_bf[1][:, halves[h], :], in_=dealt[h][:, 1, :, :])
-        quant_w(0)
+        quantise_w(0)
         for h in range(2):
             nc.vector.tensor_copy(
-                out=w_bf_pair[:, :, halves[h], :].rearrange("p t m j -> p m t j"),
-                in_=dealt[h][:, 2:4, :, :].rearrange("p t m j -> p m t j"),
+                out=w_bf_pair[:, :, halves[h], :].rearrange("p t i j -> p i t j"),
+                in_=dealt[h][:, 2:4, :, :].rearrange("p t i j -> p i t j"),
             )
         project(0)
-        quant_w(1)
-        project(1)
+        for t in range(1, PACK):
+            quantise_w(t)
+            project(t)
 
-        bound_t = bank()
-        nc.tensor.transpose(bound_t[:, 0:P], bound_rows[:], ident[:])
-        hi = keep.tile([P, T // P], F32, name="hi")
-        lo = keep.tile([P, T // P], F32, name="lo")
-        nc.scalar.copy(out=hi[:], in_=bound_t[:, 0 : T // P])
-        nc.scalar.activation(out=lo[:], in_=bound_t[:, 0 : T // P], func=COPY, scale=-1.0)
-
+        bound_turned = work_bank()
+        nc.tensor.transpose(bound_turned[:, 0:P], bound_rows[:], ident[:])
+        upper = keep.tile([P, T // P], F32, name="upper")
+        lower = keep.tile([P, T // P], F32, name="lower")
+        nc.scalar.copy(out=upper[:], in_=bound_turned[:, 0 : T // P])
+        nc.scalar.activation(out=lower[:], in_=bound_turned[:, 0 : T // P], func=COPY, scale=-1.0)
 
         out_codes = keep.tile([P, T], U32, name="out_codes", align_bytes=64)
         out_plane = keep.tile([P, T], U8, name="out_plane", align_bytes=64)
         out_rows = out_0.rearrange("(p t) v -> p t v", t=PACK)
         out_words = out_1[0].rearrange("p c r -> p (c r)").bitcast(I32)
-
-        last = len(CHUNKS) - 1
-        res = [keep.tile([P, PACK, n], F32, name="res%d" % ci) for ci, (v0, n, groups) in enumerate(CHUNKS)]
+        result = [keep.tile([P, PACK, n], F32, name="result%d" % ci) for ci, (v0, n, steps) in enumerate(CHUNKS)]
 
         y_turned = [keep.tile([P, T], F32, name="y_turned%d" % t) for t in range(PACK)]
 
         def turn_y(t):
-            for h in range(T // BANK):
-                turned = bank()
+            for c0 in range(0, T, BANK):
+                bank = work_bank()
                 for b in range(BANK // P):
-                    vb = h * (BANK // P) + b
-                    nc.tensor.transpose(turned[:, P * b : P * (b + 1)], y[t][:, P * vb : P * (vb + 1)], ident[:])
+                    nc.tensor.transpose(
+                        bank[:, P * b : P * (b + 1)], y[t][:, c0 + P * b : c0 + P * (b + 1)], ident[:]
+                    )
                 nc.scalar.activation(
-                    out=y_turned[t][:, BANK * h : BANK * (h + 1)], in_=turned[:], func=COPY, scale=float(LISTS)
+                    out=y_turned[t][:, c0 : c0 + BANK], in_=bank[:], func=COPY, scale=float(LISTS)
                 )
 
-        def forward(ci, group):
-            v0, n, groups = CHUNKS[ci]
+        def clip(dst, src, block):
+            nc.vector.tensor_scalar(
+                dst, src, upper[:, block : block + 1], lower[:, block : block + 1], ALU.min, ALU.max
+            )
+
+        def forward(ci, step):
+            v0, n, steps = CHUNKS[ci]
             blocks = n // P
-            on_vector = ci == last and group[0] == 3
-            picked = {}
-            for t in group:
+            pulls = {}
+            for t in step:
+                own = own_first[t][:] if ci == 0 else own_rest[t][:, v0 - FIRST_WIDTH : v0 - FIRST_WIDTH + n]
                 for d in range(LISTS):
-                    g = ring.tile([P, n], F32, name="picked", tag="picked", bufs=8)
-                    own = own_first[t][:] if ci == 0 else own_rest[t][:, v0 - first : v0 - first + n]
+                    pull = ring.tile([P, n], F32, name="pull", tag="pull", bufs=PULL_BUFS)
                     nc.vector.tensor_tensor(
-                        g[:], y[t][:].indirect(lists[d][:, v0 // 16 : (v0 + n) // 16]), own, ALU.subtract
+                        pull[:], y[t][:].indirect(lists[d][:, v0 // 16 : (v0 + n) // 16]), own, ALU.subtract
                     )
-                    picked[t, d] = g
+                    pulls[t, d] = pull
             clipped = [
-                ring.tile([P, len(group), BANK], F32, name="clipped", tag="clipped", bufs=10)
+                ring.tile([P, len(step), BANK], F32, name="clipped", tag="clipped", bufs=CLIPPED_BUFS)
                 for b in range(blocks)
             ]
-            pulls = [
-                ring.tile([P, len(group), BANK], F32, name="pulls", tag="pulls", bufs=6)
+            turned = [
+                ring.tile([P, len(step), BANK], F32, name="turned", tag="turned", bufs=TURNED_BUFS)
                 for b in range(blocks)
             ]
-            staged = LISTS - 1 if on_vector else LISTS
-            for i, t in enumerate(group):
+            final_step = ci == LAST and step == steps[-1]
+            staged = LISTS - 1 if final_step else LISTS
+            for i, t in enumerate(step):
                 for b in range(blocks):
-                    u = bank()
+                    bank = work_bank()
                     for d in range(staged):
-                        nc.tensor.transpose(u[:, P * d : P * (d + 1)], picked[t, d][:, P * b : P * (b + 1)], ident[:])
-                    nc.scalar.copy(out=pulls[b][:, i, 0 : P * staged], in_=u[:, 0 : P * staged])
+                        nc.tensor.transpose(bank[:, P * d : P * (d + 1)], pulls[t, d][:, P * b : P * (b + 1)], ident[:])
+                    nc.scalar.copy(out=turned[b][:, i, 0 : P * staged], in_=bank[:, 0 : P * staged])
                 if ci == 0:
                     turn_y(t)
+            width = len(step) * P * staged
             for b in range(blocks):
-                vb = v0 // P + b
-                nc.vector.tensor_scalar(
-                    clipped[b][:].rearrange("p i c -> p (i c)")[:, 0 : len(group) * P * staged],
-                    pulls[b][:].rearrange("p i c -> p (i c)")[:, 0 : len(group) * P * staged],
-                    hi[:, vb : vb + 1], lo[:, vb : vb + 1], ALU.min, ALU.max,
+                clip(
+                    clipped[b][:].rearrange("p i c -> p (i c)")[:, 0:width],
+                    turned[b][:].rearrange("p i c -> p (i c)")[:, 0:width],
+                    v0 // P + b,
                 )
-            if on_vector:
-                u = bank()
-                nc.tensor.transpose(u[:, 0:P], picked[group[0], staged][:], ident[:])
-                nc.vector.tensor_scalar(
-                    clipped[0][:, 0, P * staged : BANK], u[:, 0:P],
-                    hi[:, vb : vb + 1], lo[:, vb : vb + 1], ALU.min, ALU.max,
-                )
+            if final_step:
+                bank = work_bank()
+                nc.tensor.transpose(bank[:, 0:P], pulls[step[0], staged][:], ident[:])
+                clip(clipped[0][:, 0, P * staged : BANK], bank[:, 0:P], v0 // P)
             return clipped
 
-        def backward(ci, group, clipped):
-            v0, n, groups = CHUNKS[ci]
+        def backward(ci, step, clipped):
+            v0, n, steps = CHUNKS[ci]
             blocks = n // P
-            ts = slice(group[0], group[-1] + 1)
-            total = psum.tile([P, len(group), n], F32, name="sum_bank", tag="sum_bank", bufs=3)
-            for i, t in enumerate(group):
+            for i, t in enumerate(step):
+                total = psum.tile([P, n], F32, name="sum_bank", tag="sum_bank", bufs=SUM_BANKS)
                 for b in range(blocks):
-                    vb = v0 // P + b
                     nc.tensor.matmul(
-                        total[:, i, P * b : P * (b + 1)], y_turned[t][:, P * vb : P * (vb + 1)], ident[:],
+                        total[:, P * b : P * (b + 1)], y_turned[t][:, v0 + P * b : v0 + P * (b + 1)], ident[:],
                         start=True, stop=False, is_transpose=True,
                     )
                     for d in range(LISTS):
                         nc.tensor.matmul(
-                            total[:, i, P * b : P * (b + 1)],
-                            clipped[b][:, i, P * d : P * (d + 1)], ident[:],
+                            total[:, P * b : P * (b + 1)], clipped[b][:, i, P * d : P * (d + 1)], ident[:],
                             start=False, stop=(d == LISTS - 1), is_transpose=True,
                         )
-            nc.scalar.activation(out=res[ci][:, ts, :], in_=total[:], func=COPY, scale=1.0 / LISTS)
-            nc.sync.dma_start(out=out_rows[:, ts, v0 : v0 + n], in_=res[ci][:, ts, :])
-            if group == groups[-1]:
+                nc.scalar.activation(out=result[ci][:, t, :], in_=total[:], func=COPY, scale=1.0 / LISTS)
+                nc.sync.dma_start(out=out_rows[:, t, v0 : v0 + n], in_=result[ci][:, t, :])
+            if step == steps[-1]:
                 woven = keep.tile([P, n, PACK], BF16, name="woven%d" % ci, align_bytes=64)
-                dst = woven[:].rearrange("p (c i) t -> p c t i", i=4)
-                src = res[ci][:].rearrange("p t (c i) -> p c t i", i=4)
-                if ci == last:
-                    nc.vector.tensor_copy(out=dst, in_=src)
-                else:
-                    nc.scalar.copy(out=dst, in_=src)
-                for c0, c1 in ((0, 256), (256, 384)) if n == 384 else ((0, n),):
+                for b in range(blocks):
+                    cols = slice(P * b, P * (b + 1))
+                    src = result[ci][:, :, cols].rearrange("p t c -> p c t")
+                    if ci == LAST:
+                        nc.vector.tensor_copy(out=woven[:, cols, :], in_=src)
+                    else:
+                        nc.scalar.copy(out=woven[:, cols, :], in_=src)
+                for c0, c1 in power_of_two_runs(n):
                     nc.vector.quantize_mx(
                         out=out_codes[:, v0 + c0 : v0 + c1].bitcast(FP8X4),
                         scales=out_plane[:, v0 + c0 : v0 + c1],
                         in_=woven[:, c0:c1, :].rearrange("p c t -> p (c t)"),
                     )
-                if ci >= last - 1:
-                    c0 = 0 if ci < last else v0
+                if ci >= LAST - 1:
+                    c0 = 0 if ci < LAST else v0
                     nc.sync.dma_start(
                         out=out_words[:, c0 : v0 + n], in_=out_codes[:, c0 : v0 + n].bitcast(I32)
                     )
 
-        steps = [(ci, group) for ci, (v0, n, groups) in enumerate(CHUNKS) for group in groups]
         begun = []
         finished = 0
-        for ci, group in steps:
-            begun.append((ci, group, forward(ci, group)))
-            if ci == 0 and group[0] < 2:
-                quant_w(group[0] + 2)
-                project(group[0] + 2)
-            if len(begun) - finished > (2 if ci == last else 1):
-                backward(*begun[finished])
-                finished = finished + 1
+        for ci, (v0, n, steps) in enumerate(CHUNKS):
+            for step in steps:
+                begun.append((ci, step, forward(ci, step)))
+                if len(begun) - finished > (2 if ci == LAST else 1):
+                    backward(*begun[finished])
+                    finished = finished + 1
         for item in begun[finished:]:
             backward(*item)
 
-        for q in range(4):
+        for q in range(QUADRANTS):
             queue = nc.scalar if q % 2 == 0 else nc.sync
             queue.dma_start(
                 out=out_2[0, 4 * q : 4 * q + 4, :].bitcast(I32),

from contextlib import ExitStack

import concourse.mybir as mybir
from concourse.masks import make_identity

K, T, N = 512, 1024, 512
FLOPS = 2 * K * T * N

F32 = mybir.dt.float32
BF16 = mybir.dt.bfloat16
I32 = mybir.dt.int32
U32 = mybir.dt.uint32
U16 = mybir.dt.uint16
U8 = mybir.dt.uint8
FP8X4 = mybir.dt.float8_e4m3fn_x4
FP4X4 = mybir.dt.float4_e2m1fn_x4
ALU = mybir.AluOpType
COPY = mybir.ActivationFunctionType.Copy

P = 128
PACK = 4
BANK = 512
LISTS = 4
QUADRANTS = 4

CHUNKS = [
    (0, 512, [(0, 1), (2,), (3,)]),
    (512, 384, [(0, 1), (2,), (3,)]),
    (896, 128, [(0,), (1,), (2,), (3,)]),
]
LAST = len(CHUNKS) - 1
FIRST_WIDTH = CHUNKS[0][1]

PULL_BUFS = 2 * LISTS
TURNED_BUFS = 2 * (FIRST_WIDTH // P)
CLIPPED_BUFS = TURNED_BUFS + 2
WORK_BANKS = 5
SUM_BANKS = 3


def power_of_two_runs(n):
    runs = []
    start = 0
    while start < n:
        width = 1
        while 2 * width <= n - start:
            width = 2 * width
        runs.append((start, start + width))
        start = start + width
    return runs


def tile_picked_whuber_none_lo_kernel(
    tc, x_words, x_scales, w1, bound, pos1, pos2, pos3, pos4, out_0, out_1, out_2
):
    nc = tc.nc
    with ExitStack() as ctx:
        keep = ctx.enter_context(tc.tile_pool(name="keep", bufs=1))
        ring = ctx.enter_context(tc.tile_pool(name="ring", bufs=2))
        psum = ctx.enter_context(tc.psum_pool(name="psum", bufs=1))

        w_rows = w1.rearrange("(p j) c -> p j c", j=PACK)
        w_raw = [keep.tile([P, PACK, N // 2], F32, name="w_raw%d" % h) for h in range(2)]
        for h in range(2):
            nc.sync.dma_start(out=w_raw[h][:], in_=w_rows[:, :, h * (N // 2) : (h + 1) * (N // 2)])

        x_plane = keep.tile([P, T], U8, name="x_plane", align_bytes=64)
        nc.gpsimd.memset(x_plane[:].bitcast(I32), 0)
        for q in range(QUADRANTS):
            nc.sync.dma_start(
                out=x_plane[32 * q : 32 * q + 4, :].bitcast(I32),
                in_=x_scales[0, 4 * q : 4 * q + 4, :].bitcast(I32),
            )
        x_codes = keep.tile([P, 2 * T], U8, name="x_codes", align_bytes=64)
        nc.sync.dma_start(out=x_codes[:].bitcast(I32), in_=x_words[0].bitcast(I32))

        lists = [keep.tile([P, T // 16], U16, name="list%d" % d) for d in range(LISTS)]
        nc.sync.dma_start(lists[0][:], pos1)

        bound_rows = keep.tile([P, P], F32, name="bound_rows")
        nc.vector.memset(bound_rows[:], 0.0)
        nc.sync.dma_start(lists[1][:], pos2)
        nc.sync.dma_start(lists[2][:], pos3)
        nc.sync.dma_start(lists[3][:], pos4)
        nc.sync.dma_start(
            out=bound_rows[0 : T // P, :],
            in_=bound[0:1, :].rearrange("o (c i) -> (o c) i", i=P),
        )

        ident = keep.tile([P, P], F32, name="ident")
        make_identity(nc, ident[:])

        def work_bank():
            return psum.tile([P, BANK], F32, name="work_bank", tag="work_bank", bufs=WORK_BANKS)

        w_bf = [keep.tile([P, P, PACK], BF16, name="w_bf%d" % t, align_bytes=64)[:] for t in range(2)]
        w_bf_pair = keep.tile([P, 2, P, PACK], BF16, name="w_bf_pair", align_bytes=64)
        w_bf = w_bf + [w_bf_pair[:, 0, :, :], w_bf_pair[:, 1, :, :]]
        w_codes = [keep.tile([P, P], U32, name="w_codes%d" % t, align_bytes=64) for t in range(PACK)]
        w_plane = [keep.tile([P, P], U8, name="w_plane%d" % t, align_bytes=64) for t in range(PACK)]
        dealt = [w_raw[h][:].rearrange("p j (i t) -> p t i j", t=PACK) for h in range(2)]
        halves = [slice(0, P // 2), slice(P // 2, P)]

        def quantise_w(t):
            nc.vector.quantize_mx(
                out=w_codes[t][:].bitcast(FP8X4),
                scales=w_plane[t][:],
                in_=w_bf[t].rearrange("p i j -> p (i j)"),
            )

        y = [keep.tile([P, T], F32, name="y%d" % t) for t in range(PACK)]
        own_first = [keep.tile([P, FIRST_WIDTH], F32, name="own_first%d" % t) for t in range(PACK)]
        own_rest = [keep.tile([P, T - FIRST_WIDTH], F32, name="own_rest%d" % t) for t in range(PACK)]

        def project(t):
            width = BANK // 2 if t == 0 else BANK
            for c0 in range(0, T, width):
                cols = slice(c0, c0 + width)
                acc = work_bank()
                nc.tensor.matmul_mx(
                    out=acc[:, 0:width],
                    lhsT=w_codes[t][:].bitcast(FP8X4),
                    lhsT_scale=w_plane[t][:],
                    rhs=x_codes[:, 2 * c0 : 2 * (c0 + width)].bitcast(FP4X4),
                    rhs_scale=x_plane[:, cols],
                    start=True,
                    stop=True,
                )
                if t == 0 and c0 >= FIRST_WIDTH:
                    nc.vector.tensor_copy(out=y[t][:, cols], in_=acc[:, 0:width])
                else:
                    nc.scalar.copy(out=y[t][:, cols], in_=acc[:, 0:width])
                if c0 < FIRST_WIDTH:
                    nc.scalar.copy(out=own_first[t][:, cols], in_=acc[:, 0:width])
            nc.sync.dma_start(out=own_rest[t][:], in_=y[t][:, FIRST_WIDTH:T])

        for h in range(2):
            nc.vector.tensor_copy(out=w_bf[0][:, halves[h], :], in_=dealt[h][:, 0, :, :])
            nc.scalar.copy(out=w_bf[1][:, halves[h], :], in_=dealt[h][:, 1, :, :])
        quantise_w(0)
        for h in range(2):
            nc.vector.tensor_copy(
                out=w_bf_pair[:, :, halves[h], :].rearrange("p t i j -> p i t j"),
                in_=dealt[h][:, 2:4, :, :].rearrange("p t i j -> p i t j"),
            )
        project(0)
        for t in range(1, PACK):
            quantise_w(t)
            project(t)

        bound_turned = work_bank()
        nc.tensor.transpose(bound_turned[:, 0:P], bound_rows[:], ident[:])
        upper = keep.tile([P, T // P], F32, name="upper")
        lower = keep.tile([P, T // P], F32, name="lower")
        nc.scalar.copy(out=upper[:], in_=bound_turned[:, 0 : T // P])
        nc.scalar.activation(out=lower[:], in_=bound_turned[:, 0 : T // P], func=COPY, scale=-1.0)

        out_codes = keep.tile([P, T], U32, name="out_codes", align_bytes=64)
        out_plane = keep.tile([P, T], U8, name="out_plane", align_bytes=64)
        out_rows = out_0.rearrange("(p t) v -> p t v", t=PACK)
        out_words = out_1[0].rearrange("p c r -> p (c r)").bitcast(I32)
        result = [keep.tile([P, PACK, n], F32, name="result%d" % ci) for ci, (v0, n, steps) in enumerate(CHUNKS)]

        y_turned = [keep.tile([P, T], F32, name="y_turned%d" % t) for t in range(PACK)]

        def turn_y(t):
            for c0 in range(0, T, BANK):
                bank = work_bank()
                for b in range(BANK // P):
                    nc.tensor.transpose(
                        bank[:, P * b : P * (b + 1)], y[t][:, c0 + P * b : c0 + P * (b + 1)], ident[:]
                    )
                nc.scalar.activation(
                    out=y_turned[t][:, c0 : c0 + BANK], in_=bank[:], func=COPY, scale=float(LISTS)
                )

        def clip(dst, src, block):
            nc.vector.tensor_scalar(
                dst, src, upper[:, block : block + 1], lower[:, block : block + 1], ALU.min, ALU.max
            )

        def forward(ci, step):
            v0, n, steps = CHUNKS[ci]
            blocks = n // P
            pulls = {}
            for t in step:
                own = own_first[t][:] if ci == 0 else own_rest[t][:, v0 - FIRST_WIDTH : v0 - FIRST_WIDTH + n]
                for d in range(LISTS):
                    pull = ring.tile([P, n], F32, name="pull", tag="pull", bufs=PULL_BUFS)
                    nc.vector.tensor_tensor(
                        pull[:], y[t][:].indirect(lists[d][:, v0 // 16 : (v0 + n) // 16]), own, ALU.subtract
                    )
                    pulls[t, d] = pull
            clipped = [
                ring.tile([P, len(step), BANK], F32, name="clipped", tag="clipped", bufs=CLIPPED_BUFS)
                for b in range(blocks)
            ]
            turned = [
                ring.tile([P, len(step), BANK], F32, name="turned", tag="turned", bufs=TURNED_BUFS)
                for b in range(blocks)
            ]
            final_step = ci == LAST and step == steps[-1]
            staged = LISTS - 1 if final_step else LISTS
            for i, t in enumerate(step):
                for b in range(blocks):
                    bank = work_bank()
                    for d in range(staged):
                        nc.tensor.transpose(bank[:, P * d : P * (d + 1)], pulls[t, d][:, P * b : P * (b + 1)], ident[:])
                    nc.scalar.copy(out=turned[b][:, i, 0 : P * staged], in_=bank[:, 0 : P * staged])
                if ci == 0:
                    turn_y(t)
            width = len(step) * P * staged
            for b in range(blocks):
                clip(
                    clipped[b][:].rearrange("p i c -> p (i c)")[:, 0:width],
                    turned[b][:].rearrange("p i c -> p (i c)")[:, 0:width],
                    v0 // P + b,
                )
            if final_step:
                bank = work_bank()
                nc.tensor.transpose(bank[:, 0:P], pulls[step[0], staged][:], ident[:])
                clip(clipped[0][:, 0, P * staged : BANK], bank[:, 0:P], v0 // P)
            return clipped

        def backward(ci, step, clipped):
            v0, n, steps = CHUNKS[ci]
            blocks = n // P
            for i, t in enumerate(step):
                total = psum.tile([P, n], F32, name="sum_bank", tag="sum_bank", bufs=SUM_BANKS)
                for b in range(blocks):
                    nc.tensor.matmul(
                        total[:, P * b : P * (b + 1)], y_turned[t][:, v0 + P * b : v0 + P * (b + 1)], ident[:],
                        start=True, stop=False, is_transpose=True,
                    )
                    for d in range(LISTS):
                        nc.tensor.matmul(
                            total[:, P * b : P * (b + 1)], clipped[b][:, i, P * d : P * (d + 1)], ident[:],
                            start=False, stop=(d == LISTS - 1), is_transpose=True,
                        )
                nc.scalar.activation(out=result[ci][:, t, :], in_=total[:], func=COPY, scale=1.0 / LISTS)
                nc.sync.dma_start(out=out_rows[:, t, v0 : v0 + n], in_=result[ci][:, t, :])
            if step == steps[-1]:
                woven = keep.tile([P, n, PACK], BF16, name="woven%d" % ci, align_bytes=64)
                for b in range(blocks):
                    cols = slice(P * b, P * (b + 1))
                    src = result[ci][:, :, cols].rearrange("p t c -> p c t")
                    if ci == LAST:
                        nc.vector.tensor_copy(out=woven[:, cols, :], in_=src)
                    else:
                        nc.scalar.copy(out=woven[:, cols, :], in_=src)
                for c0, c1 in power_of_two_runs(n):
                    nc.vector.quantize_mx(
                        out=out_codes[:, v0 + c0 : v0 + c1].bitcast(FP8X4),
                        scales=out_plane[:, v0 + c0 : v0 + c1],
                        in_=woven[:, c0:c1, :].rearrange("p c t -> p (c t)"),
                    )
                if ci >= LAST - 1:
                    c0 = 0 if ci < LAST else v0
                    nc.sync.dma_start(
                        out=out_words[:, c0 : v0 + n], in_=out_codes[:, c0 : v0 + n].bitcast(I32)
                    )

        begun = []
        finished = 0
        for ci, (v0, n, steps) in enumerate(CHUNKS):
            for step in steps:
                begun.append((ci, step, forward(ci, step)))
                if len(begun) - finished > (2 if ci == LAST else 1):
                    backward(*begun[finished])
                    finished = finished + 1
        for item in begun[finished:]:
            backward(*item)

        for q in range(QUADRANTS):
            queue = nc.scalar if q % 2 == 0 else nc.sync
            queue.dma_start(
                out=out_2[0, 4 * q : 4 * q + 4, :].bitcast(I32),
                in_=out_plane[32 * q : 32 * q + 4, :].bitcast(I32),
            )
